import numpy as np
import ml_dtypes


def mxq(x, axis, fmt="e4m3"):
    dtype, down = {"e4m3": (ml_dtypes.float8_e4m3fn, 7), "e5m2": (ml_dtypes.float8_e5m2, 14)}[fmt]
    v = np.moveaxis(np.asarray(x, np.float32).astype(ml_dtypes.bfloat16).astype(np.float64), axis, -1)
    blocks = v.reshape(v.shape[:-1] + (-1, 32))
    amax = np.abs(blocks).max(-1, keepdims=True)
    byte = np.maximum(np.where(amax > 0, np.frexp(amax)[1] - 1 + 127, 0) - down, 1)
    scale = np.exp2(byte - 127.0)
    codes = (blocks / scale).astype(np.float32).astype(dtype).astype(np.float64)
    return np.moveaxis((codes * scale).reshape(v.shape), -1, axis)


WIDE = False


def mx_kscale(k):
    if not WIDE:
        return np.ones(k)
    levels = np.array([10, -10, 5, -5, 0])
    if k % 512:
        return np.exp2(np.random.permutation(np.resize(levels, k // 32))).repeat(32)
    a = np.empty((k // 512, 16))
    for p in range(k // 512):
        a[p, :8] = np.random.permutation(np.resize(levels, 8))
        for g in range(8):
            far = levels[np.abs(levels - a[p, g]) >= 10]
            a[p, g + 8] = far[np.random.randint(len(far))]
    return np.exp2(a.ravel()).repeat(32)


def f64(x):
    return np.asarray(x).astype(np.float64)


def striped(idx):
    return np.tile(idx.reshape(-1, 16).T, (8, 1)).astype(np.uint16)


def unstriped(offs):
    return offs[:16].T.reshape(-1).astype(np.int64)


def pack_weight(w):
    k, n = w.shape
    w = f64(np.asarray(w, np.float32).astype(ml_dtypes.bfloat16)).reshape(k // 32, 32, n)
    amax = np.abs(w).max(1)
    byte = np.clip(np.where(amax > 0, np.frexp(amax)[1] - 1 + 127 - 7, 1), 1, 254)
    scaled = (w * np.exp2(127.0 - byte)[:, None, :]).reshape(k, n).astype(np.float32)
    words = np.ascontiguousarray(scaled.reshape(k // 512, 128, 4, n).transpose(0, 1, 3, 2)).astype(ml_dtypes.float8_e4m3fn).view(np.uint8)
    return words, np.ascontiguousarray(byte.astype(np.uint8).reshape(k // 512, 16, n))


def unpack_weight(words, scales):
    g, p, n, _ = words.shape
    vals = np.ascontiguousarray(words).view(ml_dtypes.float8_e4m3fn).astype(np.float64) * np.repeat(np.exp2(scales.astype(np.float64) - 127.0), 8, axis=1)[..., None]
    return vals.transpose(0, 1, 3, 2).reshape(g * 512, n)


def relu(v):
    return np.maximum(v, 0.0)


K, T, S, N, H, U = 1024, 2048, 512, 128, 512, 512


def setup_inputs():
    n = np.random.standard_normal
    s = mx_kscale(K)[:, None]
    u = mx_kscale(H)
    packed_xT = pack_weight(n((K, T)) * s)
    return {
        "x_words": packed_xT[0],
        "x_scales": packed_xT[1],
        "w1": (n((K, H)) / np.sqrt(K) / s).astype(np.float32),
        "w2": (n((K, H)) / np.sqrt(K) / s).astype(np.float32),
        "lim": (np.random.uniform(0.0, 0.5, (H, U))).astype(np.float32),
        "dirv": (n((H, 1))).astype(np.float32),
        "unit": (np.random.uniform(0.6, 1.4, (H, 1)) * u[:, None]).astype(np.float32),
        "w3": (n((H, N)) / np.sqrt(H) / u[:, None]).astype(np.float32),
        "offs": striped(np.random.permutation(T)[:S]),
        "tok": striped(np.random.randint(0, S, U)),
        "cond": striped(np.random.randint(0, S, U)),
    }


def reference(x_words, x_scales, w1, w2, lim, dirv, unit, w3, offs, tok, cond):
    xq = unpack_weight(x_words, x_scales)[:, unstriped(offs)]
    y = mxq(f64(w1), 0, "e4m3").T @ xq
    yt = y[:, unstriped(tok)]
    yc = mxq(f64(w2), 0, "e4m3").T @ xq
    gc = yc[:, unstriped(cond)]
    al = relu(gc - f64(lim))
    vs = yt + f64(dirv) * al
    v2 = (yt) ** 2
    ms = v2.mean(axis=1, keepdims=True)
    nrm = np.sqrt(ms + 0.1)
    hid = f64(unit) * (vs / nrm)
    return mxq(f64(w3), 0, "e4m3").T @ mxq(hid, 0, "e4m3")

@@ -1,0 +1,241 @@
+from contextlib import ExitStack
+
+import concourse.mybir as mybir
+
+K, T, S, N, H, U = 1024, 2048, 512, 128, 512, 512
+FLOPS = 2 * (2 * K * H * S + H * N * U)
+
+F32 = mybir.dt.float32
+BF16 = mybir.dt.bfloat16
+I32 = mybir.dt.int32
+U32 = mybir.dt.uint32
+U16 = mybir.dt.uint16
+U8 = mybir.dt.uint8
+FP8X4 = mybir.dt.float8_e4m3fn_x4
+ALU = mybir.AluOpType
+ACT = mybir.ActivationFunctionType
+
+P = 128
+PACK = 4
+PASSES = K // (P * PACK)
+HALF = U // 2
+LIST_COLS = 16
+EPS = 0.1
+
+
+def tile_picked_ysteer_norm_p_kernel(
+    tc, x_words, x_scales, w1, w2, lim, dirv, unit, w3, offs, tok, cond, out
+):
+    nc = tc.nc
+    with ExitStack() as ctx:
+        keep = ctx.enter_context(tc.tile_pool(name="keep", bufs=1))
+        psum = ctx.enter_context(tc.psum_pool(name="psum", bufs=1))
+
+        def sb(name, shape, dtype, tag=None):
+            return keep.tile(shape, dtype, name=name, tag=tag or name, align_bytes=64)
+
+        offs_sb = sb("offs_sb", [P, S // LIST_COLS], U16)
+        tok_sb = sb("tok_sb", [P, U // LIST_COLS], U16)
+        cond_sb = sb("cond_sb", [P, U // LIST_COLS], U16)
+        xw = [sb("xw%d" % o, [P, T], I32) for o in range(PASSES)]
+        xs = sb("xs", [P, T], U8)
+        xs_stage = sb("xs_stage", [P, T // 4], I32)
+        w_raw = {(a, o): sb("w_raw%d%d" % (a, o), [P, PACK, H], F32) for a in range(2) for o in range(PASSES)}
+        lim_sb = sb("lim_sb", [P, PACK, U], F32)
+        w3_raw = sb("w3_raw", [P, PACK, N], F32)
+        gains = sb("gains", [P, 2, PACK], F32)
+        unit_sb = sb("unit_sb", [P, PACK], F32)
+        dirv_sb = sb("dirv_sb", [P, PACK], F32)
+        warm = sb("warm", [P, 1], F32)
+        warm_out = sb("warm_out", [P, 1], F32)
+
+        def load_w(a, o):
+            w = (w1, w2)[a]
+            rows = w[o * P * PACK : (o + 1) * P * PACK, :]
+            nc.sync.dma_start(out=w_raw[a, o][:], in_=rows.rearrange("(p j) c -> p j c", j=PACK))
+
+        def load_x(o):
+            nc.sync.dma_start(out=xw[o][:], in_=x_words[o].rearrange("p c r -> p (c r)").bitcast(I32))
+
+        nc.vector.memset(xs[:].bitcast(I32), 0)
+        nc.vector.memset(warm[:], 1.0)
+        nc.scalar.activation(out=warm_out[:], in_=warm[:], func=ACT.Sqrt)
+        nc.gpsimd.dma_start(out=unit_sb[:], in_=unit.rearrange("(p t) one -> p (t one)", t=PACK))
+        nc.gpsimd.dma_start(out=dirv_sb[:], in_=dirv.rearrange("(p t) one -> p (t one)", t=PACK))
+        nc.gpsimd.tensor_copy(out=gains[:, 0, :], in_=unit_sb[:])
+        nc.gpsimd.tensor_tensor(out=gains[:, 1, :], in0=unit_sb[:], in1=dirv_sb[:], op=ALU.mult)
+
+        load_w(0, 0)
+        nc.sync.dma_start(out=offs_sb[:], in_=offs)
+        for q in range(4):
+            rows = slice(32 * q, 32 * q + 4 * PASSES)
+            nc.sync.dma_start(out=xs_stage[rows, :], in_=x_scales[:, 4 * q : 4 * q + 4, :].bitcast(I32))
+            nc.vector.tensor_copy(out=xs[rows, :].bitcast(I32), in_=xs_stage[rows, :])
+        load_x(0)
+        load_w(0, 1)
+        load_x(1)
+        nc.sync.dma_start(out=tok_sb[:], in_=tok)
+        load_w(1, 0)
+        load_w(1, 1)
+        nc.sync.dma_start(out=cond_sb[:], in_=cond)
+        nc.sync.dma_start(out=lim_sb[:], in_=lim.rearrange("(p t) j -> p t j", t=PACK))
+        nc.sync.dma_start(out=w3_raw[:], in_=w3.rearrange("(p j) n -> p j n", j=PACK))
+
+        w_codes = {key: sb("w_codes%d%d" % key, [P, H], U32) for key in w_raw}
+        w_scales = {key: sb("w_scales%d%d" % key, [P, H], U8) for key in w_raw}
+
+        def cast_w(key, copy, t0, t1, tag=None):
+            bf = sb("w_bf%d%d%d" % (key + (t0,)), [P, (t1 - t0) * P * PACK], BF16, tag)
+            copy(
+                out=bf[:].rearrange("p (t m j) -> p m j t", t=t1 - t0, j=PACK),
+                in_=w_raw[key][:].rearrange("p j (m t) -> p m j t", t=PACK)[:, :, :, t0:t1],
+            )
+            return bf
+
+        def quant_w(key, bf, t0, t1):
+            cols = slice(t0 * P, t1 * P)
+            nc.vector.quantize_mx(out=w_codes[key][:, cols].bitcast(FP8X4), scales=w_scales[key][:, cols], in_=bf[:])
+
+        xg = [sb("xg%d" % o, [P, S], U32) for o in range(PASSES)]
+        xsg = sb("xsg", [P, S], U8)
+
+        def gather_x(o):
+            nc.vector.tensor_copy(out=xg[o][:], in_=xw[o][:].bitcast(U32).indirect(offs_sb[:]))
+
+        acc = {(a, t): psum.tile([P, S], F32, name="acc%d%d" % (a, t), tag="bank%d%d" % (a, t)) for a in range(2) for t in range(PACK)}
+
+        def product(a, o, t, first):
+            cols = slice(t * P, (t + 1) * P)
+            nc.tensor.matmul_mx(
+                out=acc[a, t][:],
+                lhsT=w_codes[a, o][:, cols].bitcast(FP8X4),
+                lhsT_scale=w_scales[a, o][:, cols],
+                rhs=xg[o][:].bitcast(FP8X4),
+                rhs_scale=xsg[4 * o :, :],
+                start=first,
+                stop=not first,
+            )
+
+        bf = cast_w((0, 0), nc.scalar.copy, 0, PACK)
+        nc.vector.tensor_copy(out=xsg[:], in_=xs[:].indirect(offs_sb[:]))
+        gather_x(0)
+        quant_w((0, 0), bf, 0, PACK)
+        for t in range(PACK):
+            product(0, 0, t, True)
+        bf = cast_w((0, 1), nc.vector.tensor_copy, 0, PACK)
+        quant_w((0, 1), bf, 0, PACK)
+        gather_x(1)
+        for t in range(PACK):
+            product(0, 1, t, False)
+
+        y = [sb("y%d" % t, [P, S], F32) for t in range(PACK)]
+        neg_yc = [sb("neg_yc%d" % t, [P, S], F32) for t in range(PACK)]
+        yt = {}
+        squares = sb("squares", [P, U], BF16)
+        sumsq = sb("sumsq", [P, PACK], F32)
+        nrm = sb("nrm", [P, PACK], F32)
+        inv = sb("inv", [P, PACK], F32)
+        factors = sb("factors", [P, 2, PACK], F32)
+
+        def list_half(lst, h):
+            return lst[:, h * HALF // LIST_COLS : (h + 1) * HALF // LIST_COLS]
+
+        def gather_y(t, tag=None):
+            yt[t] = sb("yt%d" % t, [P, U], F32, tag)
+            for h in range(2):
+                nc.vector.tensor_copy(
+                    out=yt[t][:, h * HALF : (h + 1) * HALF], in_=y[t][:].indirect(list_half(tok_sb, h))
+                )
+
+        for t in range(PACK):
+            nc.scalar.copy(out=y[t][:], in_=acc[0, t][:])
+        bf0 = cast_w((1, 0), nc.scalar.copy, 0, PACK, "w_codes01")
+        gather_y(0)
+        gather_y(1)
+        bf1a = cast_w((1, 1), nc.vector.tensor_copy, 0, 2)
+        bf1b = cast_w((1, 1), nc.scalar.copy, 2, PACK)
+        quant_w((1, 1), bf1a, 0, 2)
+        gather_y(2, "w_bf110")
+        for t in range(2):
+            product(1, 1, t, True)
+        quant_w((1, 0), bf0, 0, PACK)
+        for t in range(PACK):
+            product(1, 0, t, t >= 2)
+        gather_y(3, "w_codes01")
+        quant_w((1, 1), bf1b, 2, PACK)
+        for t in range(2, PACK):
+            product(1, 1, t, False)
+        for t in range(PACK):
+            nc.scalar.activation(out=neg_yc[t][:], in_=acc[1, t][:], func=ACT.Copy, scale=-1.0)
+        late_squares = sb("late_squares", [P, U], BF16, "w_codes11")
+        for t in range(PACK):
+            junk = squares if t < 2 else late_squares
+            nc.scalar.activation(out=junk[:], in_=yt[t][:], func=ACT.Square, accum_out=sumsq[:, t : t + 1])
+        nc.scalar.activation(out=nrm[:], in_=sumsq[:], func=ACT.Sqrt, scale=1.0 / U, bias=EPS)
+
+
+        short = [[sb("short%d%d" % (h, t), [P, HALF], F32) for t in range(PACK)] for h in range(2)]
+        steer = [[sb("steer%d%d" % (h, t), [P, HALF], F32) for t in range(PACK)] for h in range(2)]
+        hid = [sb("hid%d" % h, [P, PACK, HALF], F32) for h in range(2)]
+        hid_bf = [sb("hid_bf%d" % h, [P, HALF * PACK], BF16) for h in range(2)]
+        hid_codes = [sb("hid_codes%d" % h, [P, HALF], U32) for h in range(2)]
+        hid_scales = [sb("hid_scales%d" % h, [P, HALF], U8) for h in range(2)]
+        result = [sb("result%d" % h, [P, HALF], F32) for h in range(2)]
+        w3_codes = sb("w3_codes", [P, N], U32)
+        w3_scales = sb("w3_scales", [P, N], U8)
+
+        for h in range(2):
+            for t in range(PACK):
+                nc.vector.tensor_tensor(
+                    out=short[h][t][:],
+                    in0=neg_yc[t][:].indirect(list_half(cond_sb, h)),
+                    in1=lim_sb[:, t, h * HALF : (h + 1) * HALF],
+                    op=ALU.add,
+                )
+
+        w3_bf = sb("w3_bf", [P, N * PACK], BF16, "neg_yc0")
+        nc.scalar.copy(
+            out=w3_bf[:].rearrange("p (c i j) -> p c j i", i=4, j=PACK),
+            in_=w3_raw[:].rearrange("p j (c i) -> p c j i", i=4),
+        )
+        nc.vector.reciprocal(out=inv[:], in_=nrm[:])
+        nc.vector.quantize_mx(out=w3_codes[:].bitcast(FP8X4), scales=w3_scales[:], in_=w3_bf[:])
+        nc.vector.tensor_tensor(
+            out=factors[:], in0=gains[:], in1=inv[:].unsqueeze(1).to_broadcast([P, 2, PACK]), op=ALU.mult
+        )
+
+        def finish(h, copy):
+            for t in range(PACK):
+                nc.vector.tensor_scalar(
+                    out=steer[h][t][:], in0=short[h][t][:], scalar1=0.0, scalar2=factors[:, 1, t : t + 1],
+                    op0=ALU.min, op1=ALU.mult,
+                )
+            for t in range(PACK):
+                nc.vector.scalar_tensor_tensor(
+                    out=hid[h][:, t, :], in0=yt[t][:, h * HALF : (h + 1) * HALF], scalar=factors[:, 0, t : t + 1],
+                    in1=steer[h][t][:], op0=ALU.mult, op1=ALU.subtract,
+                )
+            copy(
+                out=hid_bf[h][:].rearrange("p (c i t) -> p c t i", i=4, t=PACK),
+                in_=hid[h][:].rearrange("p t (c i) -> p c t i", i=4),
+            )
+
+        def read_out(h):
+            nc.vector.quantize_mx(out=hid_codes[h][:].bitcast(FP8X4), scales=hid_scales[h][:], in_=hid_bf[h][:])
+            bank = psum.tile([P, HALF], F32, name="out_acc%d" % h, tag="bank0%d" % h)
+            nc.tensor.matmul_mx(
+                out=bank[:],
+                lhsT=w3_codes[:].bitcast(FP8X4),
+                lhsT_scale=w3_scales[:],
+                rhs=hid_codes[h][:].bitcast(FP8X4),
+                rhs_scale=hid_scales[h][:],
+                start=True,
+                stop=True,
+            )
+            nc.scalar.copy(out=result[h][:], in_=bank[:])
+            nc.sync.dma_start(out=out[:, h * HALF : (h + 1) * HALF], in_=result[h][:])
+
+        finish(0, nc.scalar.copy)
+        finish(1, nc.vector.tensor_copy)
+        read_out(0)
+        read_out(1)

@@ -21,6 +21,8 @@ PASSES = K // (P * PACK)
 HALF = U // 2
 LIST_COLS = 16
 EPS = 0.1
+Y_WINDOW = 704
+YC_WINDOW = 528
 
 
 def tile_picked_ysteer_norm_p_kernel(
@@ -46,6 +48,10 @@ def tile_picked_ysteer_norm_p_kernel(
         gains = sb("gains", [P, 2, PACK], F32)
         unit_sb = sb("unit_sb", [P, PACK], F32)
         dirv_sb = sb("dirv_sb", [P, PACK], F32)
+        push = sb("push", [P, PACK], F32)
+        upward = sb("upward", [P, PACK], F32)
+        sign = sb("sign", [P, PACK], F32)
+        neg_sign = sb("neg_sign", [P, PACK], F32)
         warm = sb("warm", [P, 1], F32)
         warm_out = sb("warm_out", [P, 1], F32)
 
@@ -62,8 +68,12 @@ def tile_picked_ysteer_norm_p_kernel(
         nc.scalar.activation(out=warm_out[:], in_=warm[:], func=ACT.Sqrt)
         nc.gpsimd.dma_start(out=unit_sb[:], in_=unit.rearrange("(p t) one -> p (t one)", t=PACK))
         nc.gpsimd.dma_start(out=dirv_sb[:], in_=dirv.rearrange("(p t) one -> p (t one)", t=PACK))
-        nc.gpsimd.tensor_copy(out=gains[:, 0, :], in_=unit_sb[:])
-        nc.gpsimd.tensor_tensor(out=gains[:, 1, :], in0=unit_sb[:], in1=dirv_sb[:], op=ALU.mult)
+        nc.gpsimd.tensor_tensor(out=push[:], in0=unit_sb[:], in1=dirv_sb[:], op=ALU.mult)
+        nc.gpsimd.tensor_scalar(out=upward[:], in0=push[:], scalar1=0.0, scalar2=1.0, op0=ALU.is_ge, op1=ALU.mult)
+        nc.gpsimd.tensor_scalar(out=sign[:], in0=upward[:], scalar1=2.0, scalar2=-1.0, op0=ALU.mult, op1=ALU.add)
+        nc.gpsimd.tensor_scalar(out=neg_sign[:], in0=upward[:], scalar1=-2.0, scalar2=1.0, op0=ALU.mult, op1=ALU.add)
+        nc.gpsimd.tensor_tensor(out=gains[:, 0, :], in0=unit_sb[:], in1=sign[:], op=ALU.mult)
+        nc.gpsimd.tensor_tensor(out=gains[:, 1, :], in0=push[:], in1=neg_sign[:], op=ALU.mult)
 
         load_w(0, 0)
         nc.sync.dma_start(out=offs_sb[:], in_=offs)
@@ -74,15 +84,15 @@ def tile_picked_ysteer_norm_p_kernel(
         load_x(0)
         load_w(0, 1)
         load_x(1)
+        nc.sync.dma_start(out=w3_raw[:], in_=w3.rearrange("(p j) n -> p j n", j=PACK))
         nc.sync.dma_start(out=tok_sb[:], in_=tok)
         load_w(1, 0)
         load_w(1, 1)
         nc.sync.dma_start(out=cond_sb[:], in_=cond)
         nc.sync.dma_start(out=lim_sb[:], in_=lim.rearrange("(p t) j -> p t j", t=PACK))
-        nc.sync.dma_start(out=w3_raw[:], in_=w3.rearrange("(p j) n -> p j n", j=PACK))
 
-        w_codes = {key: sb("w_codes%d%d" % key, [P, H], U32) for key in w_raw}
-        w_scales = {key: sb("w_scales%d%d" % key, [P, H], U8) for key in w_raw}
+        HP = PACK // 2
+        w_codes, w_scales = {}, {}
 
         def cast_w(key, copy, t0, t1, tag=None):
             bf = sb("w_bf%d%d%d" % (key + (t0,)), [P, (t1 - t0) * P * PACK], BF16, tag)
@@ -92,150 +102,174 @@ def tile_picked_ysteer_norm_p_kernel(
             )
             return bf
 
-        def quant_w(key, bf, t0, t1):
-            cols = slice(t0 * P, t1 * P)
-            nc.vector.quantize_mx(out=w_codes[key][:, cols].bitcast(FP8X4), scales=w_scales[key][:, cols], in_=bf[:])
+        def quant_w(key, bf, t0, t1, tag=None):
+            codes = sb("w_codes%d%d%d" % (key + (t0,)), [P, (t1 - t0) * P], U32, tag)
+            scales = sb("w_scales%d%d%d" % (key + (t0,)), [P, (t1 - t0) * P], U8)
+            nc.vector.quantize_mx(out=codes[:].bitcast(FP8X4), scales=scales[:], in_=bf)
+            for t in range(t0, t1):
+                cols = slice((t - t0) * P, (t - t0 + 1) * P)
+                w_codes[key + (t,)] = codes[:, cols]
+                w_scales[key + (t,)] = scales[:, cols]
 
         xg = [sb("xg%d" % o, [P, S], U32) for o in range(PASSES)]
         xsg = sb("xsg", [P, S], U8)
 
-        def gather_x(o):
-            nc.vector.tensor_copy(out=xg[o][:], in_=xw[o][:].bitcast(U32).indirect(offs_sb[:]))
+        def list_half(lst, h):
+            return lst[:, h * HALF // LIST_COLS : (h + 1) * HALF // LIST_COLS]
 
-        acc = {(a, t): psum.tile([P, S], F32, name="acc%d%d" % (a, t), tag="bank%d%d" % (a, t)) for a in range(2) for t in range(PACK)}
-
-        def product(a, o, t, first):
-            cols = slice(t * P, (t + 1) * P)
+        def product(acc, a, o, t, cols, first):
             nc.tensor.matmul_mx(
-                out=acc[a, t][:],
-                lhsT=w_codes[a, o][:, cols].bitcast(FP8X4),
-                lhsT_scale=w_scales[a, o][:, cols],
-                rhs=xg[o][:].bitcast(FP8X4),
-                rhs_scale=xsg[4 * o :, :],
+                out=acc[:],
+                lhsT=w_codes[a, o, t].bitcast(FP8X4),
+                lhsT_scale=w_scales[a, o, t],
+                rhs=xg[o][:, cols].bitcast(FP8X4),
+                rhs_scale=xsg[4 * o :, cols],
                 start=first,
                 stop=not first,
             )
 
+        halves = [slice(h * HALF, (h + 1) * HALF) for h in range(2)]
+        y_acc = {(t, h): psum.tile([P, HALF], F32, name="y_acc%d%d" % (t, h), tag="bank%d" % (2 * t + h)) for t in range(PACK) for h in range(2)}
+
         bf = cast_w((0, 0), nc.scalar.copy, 0, PACK)
         nc.vector.tensor_copy(out=xsg[:], in_=xs[:].indirect(offs_sb[:]))
-        gather_x(0)
-        quant_w((0, 0), bf, 0, PACK)
+        nc.vector.tensor_copy(out=xg[0][:], in_=xw[0][:].bitcast(U32).indirect(offs_sb[:]))
+        quant_w((0, 0), bf[:], 0, PACK, "xs_stage")
         for t in range(PACK):
-            product(0, 0, t, True)
-        bf = cast_w((0, 1), nc.vector.tensor_copy, 0, PACK)
-        quant_w((0, 1), bf, 0, PACK)
-        gather_x(1)
-        for t in range(PACK):
-            product(0, 1, t, False)
+            for h in range(2):
+                product(y_acc[t, h], 0, 0, t, halves[h], True)
+        bf_low = cast_w((0, 1), nc.vector.tensor_copy, 0, HP, "w_bf000")
+        bf_high = cast_w((0, 1), nc.scalar.copy, HP, PACK)
+        quant_w((0, 1), bf_low[:], 0, HP)
+        quant_w((0, 1), bf_high[:], HP, PACK)
+        for h in range(2):
+            nc.vector.tensor_copy(out=xg[1][:, halves[h]], in_=xw[1][:].bitcast(U32).indirect(list_half(offs_sb, h)))
 
-        y = [sb("y%d" % t, [P, S], F32) for t in range(PACK)]
-        neg_yc = [sb("neg_yc%d" % t, [P, S], F32) for t in range(PACK)]
+        w3_bf = sb("w3_bf", [P, N, PACK], BF16, "xw1")
+        w3_codes = sb("w3_codes", [P, N], U32)
+        w3_scales = sb("w3_scales", [P, N], U8)
+        nc.vector.tensor_tensor(
+            out=w3_bf[:],
+            in0=w3_raw[:].rearrange("p j n -> p n j"),
+            in1=sign[:].unsqueeze(1).to_broadcast([P, N, PACK]),
+            op=ALU.mult,
+        )
+        nc.vector.quantize_mx(
+            out=w3_codes[:].bitcast(FP8X4), scales=w3_scales[:], in_=w3_bf[:].rearrange("p n j -> p (n j)")
+        )
+
+        y = [sb("y%d" % t, [P, Y_WINDOW], F32) for t in range(PACK)]
+        neg_yc = [sb("neg_yc%d" % t, [P, YC_WINDOW], F32) for t in range(PACK)]
+        for window in y + neg_yc:
+            nc.gpsimd.memset(window[:, S:], 0.0)
         yt = {}
-        squares = sb("squares", [P, U], BF16)
         sumsq = sb("sumsq", [P, PACK], F32)
         nrm = sb("nrm", [P, PACK], F32)
         inv = sb("inv", [P, PACK], F32)
         factors = sb("factors", [P, 2, PACK], F32)
 
-        def list_half(lst, h):
-            return lst[:, h * HALF // LIST_COLS : (h + 1) * HALF // LIST_COLS]
+        def finish_y(t0):
+            for h in range(2):
+                for t in range(t0, t0 + HP):
+                    product(y_acc[t, h], 0, 1, t, halves[h], False)
+                    nc.scalar.copy(out=y[t][:, halves[h]], in_=y_acc[t, h][:])
 
         def gather_y(t, tag=None):
             yt[t] = sb("yt%d" % t, [P, U], F32, tag)
-            for h in range(2):
-                nc.vector.tensor_copy(
-                    out=yt[t][:, h * HALF : (h + 1) * HALF], in_=y[t][:].indirect(list_half(tok_sb, h))
-                )
+            nc.vector.tensor_copy(out=yt[t][:], in_=y[t][:].indirect(tok_sb[:]))
 
-        for t in range(PACK):
-            nc.scalar.copy(out=y[t][:], in_=acc[0, t][:])
-        bf0 = cast_w((1, 0), nc.scalar.copy, 0, PACK, "w_codes01")
-        gather_y(0)
+        whole = slice(0, S)
+        finish_y(0)
+        bf0 = cast_w((1, 0), nc.scalar.copy, 0, PACK, "w_codes010")
+        finish_y(HP)
+        gather_y(0, "xw1")
         gather_y(1)
-        bf1a = cast_w((1, 1), nc.vector.tensor_copy, 0, 2)
-        bf1b = cast_w((1, 1), nc.scalar.copy, 2, PACK)
-        quant_w((1, 1), bf1a, 0, 2)
-        gather_y(2, "w_bf110")
-        for t in range(2):
-            product(1, 1, t, True)
-        quant_w((1, 0), bf0, 0, PACK)
+        bf1a = cast_w((1, 1), nc.vector.tensor_copy, 0, HP, "y1")
+        bf1b = cast_w((1, 1), nc.scalar.copy, HP, PACK, "w_raw10")
+        yc_acc = [psum.tile([P, S], F32, name="yc_acc%d" % t, tag="bank%d" % t) for t in range(PACK)]
+        quant_w((1, 1), bf1a[:], 0, HP)
+        for t in range(HP):
+            product(yc_acc[t], 1, 1, t, whole, True)
+        quant_w((1, 0), bf0[:], 0, PACK)
         for t in range(PACK):
-            product(1, 0, t, t >= 2)
-        gather_y(3, "w_codes01")
-        quant_w((1, 1), bf1b, 2, PACK)
-        for t in range(2, PACK):
-            product(1, 1, t, False)
+            product(yc_acc[t], 1, 0, t, whole, t >= HP)
+        gather_y(2, "y1")
+        quant_w((1, 1), bf1b[:], HP, PACK)
+        gather_y(3, "w_raw10")
+        for t in range(HP, PACK):
+            product(yc_acc[t], 1, 1, t, whole, False)
         for t in range(PACK):
-            nc.scalar.activation(out=neg_yc[t][:], in_=acc[1, t][:], func=ACT.Copy, scale=-1.0)
-        late_squares = sb("late_squares", [P, U], BF16, "w_codes11")
+            nc.scalar.activation(out=neg_yc[t][:, :S], in_=yc_acc[t][:], func=ACT.Copy, scale=-1.0)
+        squares = sb("squares", [P, U], BF16, "w_raw11")
+        late_squares = sb("late_squares", [P, U], BF16, "w_codes112")
         for t in range(PACK):
             junk = squares if t < 2 else late_squares
             nc.scalar.activation(out=junk[:], in_=yt[t][:], func=ACT.Square, accum_out=sumsq[:, t : t + 1])
         nc.scalar.activation(out=nrm[:], in_=sumsq[:], func=ACT.Sqrt, scale=1.0 / U, bias=EPS)
 
-
-        short = [[sb("short%d%d" % (h, t), [P, HALF], F32) for t in range(PACK)] for h in range(2)]
-        steer = [[sb("steer%d%d" % (h, t), [P, HALF], F32) for t in range(PACK)] for h in range(2)]
+        steer = [sb("steer%d" % t, [P, U], F32) for t in range(PACK)]
         hid = [sb("hid%d" % h, [P, PACK, HALF], F32) for h in range(2)]
-        hid_bf = [sb("hid_bf%d" % h, [P, HALF * PACK], BF16) for h in range(2)]
-        hid_codes = [sb("hid_codes%d" % h, [P, HALF], U32) for h in range(2)]
-        hid_scales = [sb("hid_scales%d" % h, [P, HALF], U8) for h in range(2)]
-        result = [sb("result%d" % h, [P, HALF], F32) for h in range(2)]
-        w3_codes = sb("w3_codes", [P, N], U32)
-        w3_scales = sb("w3_scales", [P, N], U8)
 
-        for h in range(2):
-            for t in range(PACK):
-                nc.vector.tensor_tensor(
-                    out=short[h][t][:],
-                    in0=neg_yc[t][:].indirect(list_half(cond_sb, h)),
-                    in1=lim_sb[:, t, h * HALF : (h + 1) * HALF],
-                    op=ALU.add,
-                )
+        short = {}
 
-        w3_bf = sb("w3_bf", [P, N * PACK], BF16, "neg_yc0")
-        nc.scalar.copy(
-            out=w3_bf[:].rearrange("p (c i j) -> p c j i", i=4, j=PACK),
-            in_=w3_raw[:].rearrange("p j (c i) -> p c j i", i=4),
-        )
+        def gather_short(t, tag=None):
+            short[t] = sb("short%d" % t, [P, U], F32, tag)
+            nc.vector.tensor_tensor(
+                out=short[t][:], in0=neg_yc[t][:].indirect(cond_sb[:]), in1=lim_sb[:, t, :], op=ALU.add
+            )
+
+        LAST = PACK - 1
+        gather_short(0, "y3")
+        gather_short(1)
+        gather_short(2)
         nc.vector.reciprocal(out=inv[:], in_=nrm[:])
-        nc.vector.quantize_mx(out=w3_codes[:].bitcast(FP8X4), scales=w3_scales[:], in_=w3_bf[:])
         nc.vector.tensor_tensor(
             out=factors[:], in0=gains[:], in1=inv[:].unsqueeze(1).to_broadcast([P, 2, PACK]), op=ALU.mult
         )
-
-        def finish(h, copy):
-            for t in range(PACK):
-                nc.vector.tensor_scalar(
-                    out=steer[h][t][:], in0=short[h][t][:], scalar1=0.0, scalar2=factors[:, 1, t : t + 1],
-                    op0=ALU.min, op1=ALU.mult,
-                )
+        gather_short(LAST, "inv")
+        for t in range(LAST):
+            nc.scalar.activation(out=steer[t][:], in_=short[t][:], func=ACT.Relu, scale=factors[:, 1, t : t + 1])
+        nc.vector.tensor_scalar(
+            out=steer[LAST][:], in0=short[LAST][:], scalar1=0.0, scalar2=factors[:, 1, LAST:],
+            op0=ALU.min, op1=ALU.mult,
+        )
+        for h in range(2):
             for t in range(PACK):
                 nc.vector.scalar_tensor_tensor(
-                    out=hid[h][:, t, :], in0=yt[t][:, h * HALF : (h + 1) * HALF], scalar=factors[:, 0, t : t + 1],
-                    in1=steer[h][t][:], op0=ALU.mult, op1=ALU.subtract,
+                    out=hid[h][:, t, :], in0=yt[t][:, halves[h]], scalar=factors[:, 0, t : t + 1],
+                    in1=steer[t][:, halves[h]], op0=ALU.mult, op1=ALU.add,
                 )
-            copy(
-                out=hid_bf[h][:].rearrange("p (c i t) -> p c t i", i=4, t=PACK),
-                in_=hid[h][:].rearrange("p t (c i) -> p c t i", i=4),
-            )
 
-        def read_out(h):
-            nc.vector.quantize_mx(out=hid_codes[h][:].bitcast(FP8X4), scales=hid_scales[h][:], in_=hid_bf[h][:])
-            bank = psum.tile([P, HALF], F32, name="out_acc%d" % h, tag="bank0%d" % h)
+        def interleave(n, h, c0, c1, copy):
+            bf = sb("hid_bf%d" % n, [P, (c1 - c0) * PACK], BF16)
+            copy(
+                out=bf[:].rearrange("p (c i t) -> p c t i", i=4, t=PACK),
+                in_=hid[h][:, :, c0:c1].rearrange("p t (c i) -> p c t i", i=4),
+            )
+            return bf
+
+        def read_out(n, bf, j0, width, copy, queue):
+            codes = sb("hid_codes%d" % n, [P, width], U32)
+            scales = sb("hid_scales%d" % n, [P, width], U8)
+            result = sb("result%d" % n, [P, width], F32)
+            nc.vector.quantize_mx(out=codes[:].bitcast(FP8X4), scales=scales[:], in_=bf[:])
+            bank = psum.tile([P, width], F32, name="out_acc%d" % n, tag="bank%d" % (PACK + n))
             nc.tensor.matmul_mx(
                 out=bank[:],
                 lhsT=w3_codes[:].bitcast(FP8X4),
                 lhsT_scale=w3_scales[:],
-                rhs=hid_codes[h][:].bitcast(FP8X4),
-                rhs_scale=hid_scales[h][:],
+                rhs=codes[:].bitcast(FP8X4),
+                rhs_scale=scales[:],
                 start=True,
                 stop=True,
             )
-            nc.scalar.copy(out=result[h][:], in_=bank[:])
-            nc.sync.dma_start(out=out[:, h * HALF : (h + 1) * HALF], in_=result[h][:])
+            copy(out=result[:], in_=bank[:])
+            queue.dma_start(out=out[:, j0 : j0 + width], in_=result[:])
 
-        finish(0, nc.scalar.copy)
-        finish(1, nc.vector.tensor_copy)
-        read_out(0)
-        read_out(1)
+        QUARTER = HALF // 2
+        bf_a = interleave(0, 0, 0, HALF, nc.scalar.copy)
+        bf_b = interleave(1, 1, 0, QUARTER, nc.scalar.copy)
+        bf_c = interleave(2, 1, QUARTER, HALF, nc.vector.tensor_copy)
+        read_out(0, bf_a, 0, HALF, nc.scalar.copy, nc.sync)
+        read_out(2, bf_c, HALF + QUARTER, QUARTER, nc.scalar.copy, nc.sync)
+        read_out(1, bf_b, HALF, QUARTER, nc.vector.tensor_copy, nc.sync)

from contextlib import ExitStack

import concourse.mybir as mybir

K, T, S, N, H, U = 1024, 2048, 512, 128, 512, 512
FLOPS = 2 * (2 * K * H * S + H * N * U)

F32 = mybir.dt.float32
BF16 = mybir.dt.bfloat16
I32 = mybir.dt.int32
U32 = mybir.dt.uint32
U16 = mybir.dt.uint16
U8 = mybir.dt.uint8
FP8X4 = mybir.dt.float8_e4m3fn_x4
ALU = mybir.AluOpType
ACT = mybir.ActivationFunctionType

P = 128
PACK = 4
PASSES = K // (P * PACK)
HALF = U // 2
LIST_COLS = 16
EPS = 0.1
Y_WINDOW = 704
YC_WINDOW = 528


def tile_picked_ysteer_norm_p_kernel(
    tc, x_words, x_scales, w1, w2, lim, dirv, unit, w3, offs, tok, cond, out
):
    nc = tc.nc
    with ExitStack() as ctx:
        keep = ctx.enter_context(tc.tile_pool(name="keep", bufs=1))
        psum = ctx.enter_context(tc.psum_pool(name="psum", bufs=1))

        def sb(name, shape, dtype, tag=None):
            return keep.tile(shape, dtype, name=name, tag=tag or name, align_bytes=64)

        offs_sb = sb("offs_sb", [P, S // LIST_COLS], U16)
        tok_sb = sb("tok_sb", [P, U // LIST_COLS], U16)
        cond_sb = sb("cond_sb", [P, U // LIST_COLS], U16)
        xw = [sb("xw%d" % o, [P, T], I32) for o in range(PASSES)]
        xs = sb("xs", [P, T], U8)
        xs_stage = sb("xs_stage", [P, T // 4], I32)
        w_raw = {(a, o): sb("w_raw%d%d" % (a, o), [P, PACK, H], F32) for a in range(2) for o in range(PASSES)}
        lim_sb = sb("lim_sb", [P, PACK, U], F32)
        w3_raw = sb("w3_raw", [P, PACK, N], F32)
        gains = sb("gains", [P, 2, PACK], F32)
        unit_sb = sb("unit_sb", [P, PACK], F32)
        dirv_sb = sb("dirv_sb", [P, PACK], F32)
        push = sb("push", [P, PACK], F32)
        upward = sb("upward", [P, PACK], F32)
        sign = sb("sign", [P, PACK], F32)
        neg_sign = sb("neg_sign", [P, PACK], F32)
        warm = sb("warm", [P, 1], F32)
        warm_out = sb("warm_out", [P, 1], F32)

        def load_w(a, o):
            w = (w1, w2)[a]
            rows = w[o * P * PACK : (o + 1) * P * PACK, :]
            nc.sync.dma_start(out=w_raw[a, o][:], in_=rows.rearrange("(p j) c -> p j c", j=PACK))

        def load_x(o):
            nc.sync.dma_start(out=xw[o][:], in_=x_words[o].rearrange("p c r -> p (c r)").bitcast(I32))

        nc.vector.memset(xs[:].bitcast(I32), 0)
        nc.vector.memset(warm[:], 1.0)
        nc.scalar.activation(out=warm_out[:], in_=warm[:], func=ACT.Sqrt)
        nc.gpsimd.dma_start(out=unit_sb[:], in_=unit.rearrange("(p t) one -> p (t one)", t=PACK))
        nc.gpsimd.dma_start(out=dirv_sb[:], in_=dirv.rearrange("(p t) one -> p (t one)", t=PACK))
        nc.gpsimd.tensor_tensor(out=push[:], in0=unit_sb[:], in1=dirv_sb[:], op=ALU.mult)
        nc.gpsimd.tensor_scalar(out=upward[:], in0=push[:], scalar1=0.0, scalar2=1.0, op0=ALU.is_ge, op1=ALU.mult)
        nc.gpsimd.tensor_scalar(out=sign[:], in0=upward[:], scalar1=2.0, scalar2=-1.0, op0=ALU.mult, op1=ALU.add)
        nc.gpsimd.tensor_scalar(out=neg_sign[:], in0=upward[:], scalar1=-2.0, scalar2=1.0, op0=ALU.mult, op1=ALU.add)
        nc.gpsimd.tensor_tensor(out=gains[:, 0, :], in0=unit_sb[:], in1=sign[:], op=ALU.mult)
        nc.gpsimd.tensor_tensor(out=gains[:, 1, :], in0=push[:], in1=neg_sign[:], op=ALU.mult)

        load_w(0, 0)
        nc.sync.dma_start(out=offs_sb[:], in_=offs)
        for q in range(4):
            rows = slice(32 * q, 32 * q + 4 * PASSES)
            nc.sync.dma_start(out=xs_stage[rows, :], in_=x_scales[:, 4 * q : 4 * q + 4, :].bitcast(I32))
            nc.vector.tensor_copy(out=xs[rows, :].bitcast(I32), in_=xs_stage[rows, :])
        load_x(0)
        load_w(0, 1)
        load_x(1)
        nc.sync.dma_start(out=w3_raw[:], in_=w3.rearrange("(p j) n -> p j n", j=PACK))
        nc.sync.dma_start(out=tok_sb[:], in_=tok)
        load_w(1, 0)
        load_w(1, 1)
        nc.sync.dma_start(out=cond_sb[:], in_=cond)
        nc.sync.dma_start(out=lim_sb[:], in_=lim.rearrange("(p t) j -> p t j", t=PACK))

        HP = PACK // 2
        w_codes, w_scales = {}, {}

        def cast_w(key, copy, t0, t1, tag=None):
            bf = sb("w_bf%d%d%d" % (key + (t0,)), [P, (t1 - t0) * P * PACK], BF16, tag)
            copy(
                out=bf[:].rearrange("p (t m j) -> p m j t", t=t1 - t0, j=PACK),
                in_=w_raw[key][:].rearrange("p j (m t) -> p m j t", t=PACK)[:, :, :, t0:t1],
            )
            return bf

        def quant_w(key, bf, t0, t1, tag=None):
            codes = sb("w_codes%d%d%d" % (key + (t0,)), [P, (t1 - t0) * P], U32, tag)
            scales = sb("w_scales%d%d%d" % (key + (t0,)), [P, (t1 - t0) * P], U8)
            nc.vector.quantize_mx(out=codes[:].bitcast(FP8X4), scales=scales[:], in_=bf)
            for t in range(t0, t1):
                cols = slice((t - t0) * P, (t - t0 + 1) * P)
                w_codes[key + (t,)] = codes[:, cols]
                w_scales[key + (t,)] = scales[:, cols]

        xg = [sb("xg%d" % o, [P, S], U32) for o in range(PASSES)]
        xsg = sb("xsg", [P, S], U8)

        def list_half(lst, h):
            return lst[:, h * HALF // LIST_COLS : (h + 1) * HALF // LIST_COLS]

        def product(acc, a, o, t, cols, first):
            nc.tensor.matmul_mx(
                out=acc[:],
                lhsT=w_codes[a, o, t].bitcast(FP8X4),
                lhsT_scale=w_scales[a, o, t],
                rhs=xg[o][:, cols].bitcast(FP8X4),
                rhs_scale=xsg[4 * o :, cols],
                start=first,
                stop=not first,
            )

        halves = [slice(h * HALF, (h + 1) * HALF) for h in range(2)]
        y_acc = {(t, h): psum.tile([P, HALF], F32, name="y_acc%d%d" % (t, h), tag="bank%d" % (2 * t + h)) for t in range(PACK) for h in range(2)}

        bf = cast_w((0, 0), nc.scalar.copy, 0, PACK)
        nc.vector.tensor_copy(out=xsg[:], in_=xs[:].indirect(offs_sb[:]))
        nc.vector.tensor_copy(out=xg[0][:], in_=xw[0][:].bitcast(U32).indirect(offs_sb[:]))
        quant_w((0, 0), bf[:], 0, PACK, "xs_stage")
        for t in range(PACK):
            for h in range(2):
                product(y_acc[t, h], 0, 0, t, halves[h], True)
        bf_low = cast_w((0, 1), nc.vector.tensor_copy, 0, HP, "w_bf000")
        bf_high = cast_w((0, 1), nc.scalar.copy, HP, PACK)
        quant_w((0, 1), bf_low[:], 0, HP)
        quant_w((0, 1), bf_high[:], HP, PACK)
        for h in range(2):
            nc.vector.tensor_copy(out=xg[1][:, halves[h]], in_=xw[1][:].bitcast(U32).indirect(list_half(offs_sb, h)))

        w3_bf = sb("w3_bf", [P, N, PACK], BF16, "xw1")
        w3_codes = sb("w3_codes", [P, N], U32)
        w3_scales = sb("w3_scales", [P, N], U8)
        nc.vector.tensor_tensor(
            out=w3_bf[:],
            in0=w3_raw[:].rearrange("p j n -> p n j"),
            in1=sign[:].unsqueeze(1).to_broadcast([P, N, PACK]),
            op=ALU.mult,
        )
        nc.vector.quantize_mx(
            out=w3_codes[:].bitcast(FP8X4), scales=w3_scales[:], in_=w3_bf[:].rearrange("p n j -> p (n j)")
        )

        y = [sb("y%d" % t, [P, Y_WINDOW], F32) for t in range(PACK)]
        neg_yc = [sb("neg_yc%d" % t, [P, YC_WINDOW], F32) for t in range(PACK)]
        for window in y + neg_yc:
            nc.gpsimd.memset(window[:, S:], 0.0)
        yt = {}
        sumsq = sb("sumsq", [P, PACK], F32)
        nrm = sb("nrm", [P, PACK], F32)
        inv = sb("inv", [P, PACK], F32)
        factors = sb("factors", [P, 2, PACK], F32)

        def finish_y(t0):
            for h in range(2):
                for t in range(t0, t0 + HP):
                    product(y_acc[t, h], 0, 1, t, halves[h], False)
                    nc.scalar.copy(out=y[t][:, halves[h]], in_=y_acc[t, h][:])

        def gather_y(t, tag=None):
            yt[t] = sb("yt%d" % t, [P, U], F32, tag)
            nc.vector.tensor_copy(out=yt[t][:], in_=y[t][:].indirect(tok_sb[:]))

        whole = slice(0, S)
        finish_y(0)
        bf0 = cast_w((1, 0), nc.scalar.copy, 0, PACK, "w_codes010")
        finish_y(HP)
        gather_y(0, "xw1")
        gather_y(1)
        bf1a = cast_w((1, 1), nc.vector.tensor_copy, 0, HP, "y1")
        bf1b = cast_w((1, 1), nc.scalar.copy, HP, PACK, "w_raw10")
        yc_acc = [psum.tile([P, S], F32, name="yc_acc%d" % t, tag="bank%d" % t) for t in range(PACK)]
        quant_w((1, 1), bf1a[:], 0, HP)
        for t in range(HP):
            product(yc_acc[t], 1, 1, t, whole, True)
        quant_w((1, 0), bf0[:], 0, PACK)
        for t in range(PACK):
            product(yc_acc[t], 1, 0, t, whole, t >= HP)
        gather_y(2, "y1")
        quant_w((1, 1), bf1b[:], HP, PACK)
        gather_y(3, "w_raw10")
        for t in range(HP, PACK):
            product(yc_acc[t], 1, 1, t, whole, False)
        for t in range(PACK):
            nc.scalar.activation(out=neg_yc[t][:, :S], in_=yc_acc[t][:], func=ACT.Copy, scale=-1.0)
        squares = sb("squares", [P, U], BF16, "w_raw11")
        late_squares = sb("late_squares", [P, U], BF16, "w_codes112")
        for t in range(PACK):
            junk = squares if t < 2 else late_squares
            nc.scalar.activation(out=junk[:], in_=yt[t][:], func=ACT.Square, accum_out=sumsq[:, t : t + 1])
        nc.scalar.activation(out=nrm[:], in_=sumsq[:], func=ACT.Sqrt, scale=1.0 / U, bias=EPS)

        steer = [sb("steer%d" % t, [P, U], F32) for t in range(PACK)]
        hid = [sb("hid%d" % h, [P, PACK, HALF], F32) for h in range(2)]

        short = {}

        def gather_short(t, tag=None):
            short[t] = sb("short%d" % t, [P, U], F32, tag)
            nc.vector.tensor_tensor(
                out=short[t][:], in0=neg_yc[t][:].indirect(cond_sb[:]), in1=lim_sb[:, t, :], op=ALU.add
            )

        LAST = PACK - 1
        gather_short(0, "y3")
        gather_short(1)
        gather_short(2)
        nc.vector.reciprocal(out=inv[:], in_=nrm[:])
        nc.vector.tensor_tensor(
            out=factors[:], in0=gains[:], in1=inv[:].unsqueeze(1).to_broadcast([P, 2, PACK]), op=ALU.mult
        )
        gather_short(LAST, "inv")
        for t in range(LAST):
            nc.scalar.activation(out=steer[t][:], in_=short[t][:], func=ACT.Relu, scale=factors[:, 1, t : t + 1])
        nc.vector.tensor_scalar(
            out=steer[LAST][:], in0=short[LAST][:], scalar1=0.0, scalar2=factors[:, 1, LAST:],
            op0=ALU.min, op1=ALU.mult,
        )
        for h in range(2):
            for t in range(PACK):
                nc.vector.scalar_tensor_tensor(
                    out=hid[h][:, t, :], in0=yt[t][:, halves[h]], scalar=factors[:, 0, t : t + 1],
                    in1=steer[t][:, halves[h]], op0=ALU.mult, op1=ALU.add,
                )

        def interleave(n, h, c0, c1, copy):
            bf = sb("hid_bf%d" % n, [P, (c1 - c0) * PACK], BF16)
            copy(
                out=bf[:].rearrange("p (c i t) -> p c t i", i=4, t=PACK),
                in_=hid[h][:, :, c0:c1].rearrange("p t (c i) -> p c t i", i=4),
            )
            return bf

        def read_out(n, bf, j0, width, copy, queue):
            codes = sb("hid_codes%d" % n, [P, width], U32)
            scales = sb("hid_scales%d" % n, [P, width], U8)
            result = sb("result%d" % n, [P, width], F32)
            nc.vector.quantize_mx(out=codes[:].bitcast(FP8X4), scales=scales[:], in_=bf[:])
            bank = psum.tile([P, width], F32, name="out_acc%d" % n, tag="bank%d" % (PACK + n))
            nc.tensor.matmul_mx(
                out=bank[:],
                lhsT=w3_codes[:].bitcast(FP8X4),
                lhsT_scale=w3_scales[:],
                rhs=codes[:].bitcast(FP8X4),
                rhs_scale=scales[:],
                start=True,
                stop=True,
            )
            copy(out=result[:], in_=bank[:])
            queue.dma_start(out=out[:, j0 : j0 + width], in_=result[:])

        QUARTER = HALF // 2
        bf_a = interleave(0, 0, 0, HALF, nc.scalar.copy)
        bf_b = interleave(1, 1, 0, QUARTER, nc.scalar.copy)
        bf_c = interleave(2, 1, QUARTER, HALF, nc.vector.tensor_copy)
        read_out(0, bf_a, 0, HALF, nc.scalar.copy, nc.sync)
        read_out(2, bf_c, HALF + QUARTER, QUARTER, nc.scalar.copy, nc.sync)
        read_out(1, bf_b, HALF, QUARTER, nc.vector.tensor_copy, nc.sync)
